import numpy as np
import ml_dtypes


def mxq(x, axis, fmt="e4m3"):
    dtype, down = {"e4m3": (ml_dtypes.float8_e4m3fn, 7), "e5m2": (ml_dtypes.float8_e5m2, 14)}[fmt]
    v = np.moveaxis(np.asarray(x, np.float32).astype(ml_dtypes.bfloat16).astype(np.float64), axis, -1)
    blocks = v.reshape(v.shape[:-1] + (-1, 32))
    amax = np.abs(blocks).max(-1, keepdims=True)
    byte = np.maximum(np.where(amax > 0, np.frexp(amax)[1] - 1 + 127, 0) - down, 1)
    scale = np.exp2(byte - 127.0)
    codes = (blocks / scale).astype(np.float32).astype(dtype).astype(np.float64)
    return np.moveaxis((codes * scale).reshape(v.shape), -1, axis)


WIDE = False


def mx_kscale(k):
    if not WIDE:
        return np.ones(k)
    levels = np.array([10, -10, 5, -5, 0])
    if k % 512:
        return np.exp2(np.random.permutation(np.resize(levels, k // 32))).repeat(32)
    a = np.empty((k // 512, 16))
    for p in range(k // 512):
        a[p, :8] = np.random.permutation(np.resize(levels, 8))
        for g in range(8):
            far = levels[np.abs(levels - a[p, g]) >= 10]
            a[p, g + 8] = far[np.random.randint(len(far))]
    return np.exp2(a.ravel()).repeat(32)


BF16 = ml_dtypes.bfloat16


def bf(x):
    return np.asarray(x, np.float32).astype(BF16)


def f64(x):
    return np.asarray(x).astype(np.float64)


E2M1 = np.array([0.0, 0.5, 1.0, 1.5, 2.0, 3.0, 4.0, 6.0, -0.0, -0.5, -1.0, -1.5, -2.0, -3.0, -4.0, -6.0])


def pack_weight(w, fmt):
    k, n = w.shape
    w = f64(bf(w)).reshape(k // 32, 32, n)
    amax = np.abs(w).max(1)
    if fmt == "e4m3":
        byte = np.frexp(amax)[1] - 1 + 127 - 7
    else:
        mant, ex = np.frexp(amax / 6.0)
        byte = np.where(mant > 0.5, ex, ex - 1) + 127
    byte = np.clip(np.where(amax > 0, byte, 1), 1, 254)
    scaled = (w * np.exp2(127.0 - byte)[:, None, :]).reshape(k, n).astype(np.float32)
    by_word = np.ascontiguousarray(scaled.reshape(k // 512, 128, 4, n).transpose(0, 1, 3, 2))
    if fmt == "e4m3":
        words = by_word.astype(ml_dtypes.float8_e4m3fn).view(np.uint8)
    else:
        c = by_word.astype(ml_dtypes.float4_e2m1fn).view(np.uint8) & 0xF
        words = c[..., 0::2] | (c[..., 1::2] << 4)
    return np.ascontiguousarray(words), np.ascontiguousarray(byte.astype(np.uint8).reshape(k // 512, 16, n))


def unpack_weight(words, scales, fmt):
    g, p, n, _ = words.shape
    if fmt == "e4m3":
        vals = np.ascontiguousarray(words).view(ml_dtypes.float8_e4m3fn).astype(np.float64)
    else:
        nib = np.empty((g, p, n, 4), np.uint8)
        nib[..., 0::2] = words & 0xF
        nib[..., 1::2] = words >> 4
        vals = E2M1[nib]
    vals = vals * np.repeat(np.exp2(scales.astype(np.float64) - 127.0), 8, axis=1)[..., None]
    return vals.transpose(0, 1, 3, 2).reshape(g * 512, n)
def pack4(w):
    words, scales = pack_weight(w, "e2m1")
    return words.reshape(words.shape[0], 128, -1), scales


def unpack4(words, scales):
    return unpack_weight(words.reshape(words.shape[0], 128, -1, 2), scales, "e2m1")


M, K, N, R = 1024, 2048, 1024, 512


def draw0():
    s, t, r = mx_kscale(K), mx_kscale(N), mx_kscale(M)
    x = np.random.standard_normal((M, K)) * s * r[:, None]
    v = np.random.standard_normal((K, N)) / np.sqrt(K) / s[:, None]
    mu = 0.5 * np.random.standard_normal((M, N)) * r[:, None]
    gain = (1 + 0.1 * np.random.standard_normal(N)) * t
    u = np.random.standard_normal((R, M)) / np.sqrt(M) / r
    b_words, b_scales = pack4(np.random.standard_normal((N, K)) / np.sqrt(N) / t[:, None])
    return {"x": bf(x), "v": bf(v), "mu": bf(mu), "gain": bf(gain), "u": bf(u),
            "b_words": b_words, "b_scales": b_scales}


def core(x, v, mu, gain, u, b_words, b_scales):
    y = mxq(f64(x), 1, "e4m3") @ mxq(f64(v), 0, "e4m3")
    h = (y - f64(mu)) * f64(gain)
    c = mxq(f64(u), 1, "e4m3") @ mxq(h, 0, "e4m3")
    z = mxq(h, 1, "e4m3") @ unpack4(b_words, b_scales)
    return c, z


def e4m3fn_bytes(y):
    return np.clip(np.asarray(y, np.float64), -448.0, 448.0).astype(np.float32).astype(ml_dtypes.float8_e4m3fn).view(np.uint8)


def e4m3fn_values(b):
    return np.asarray(b, np.uint8).view(ml_dtypes.float8_e4m3fn).astype(np.float64)


def setup_inputs():
    d = draw0()
    x0 = np.asarray(d['v']).astype(np.float64)
    s = (np.max(np.abs(x0), axis=(1,), keepdims=True) / 448.0).astype(np.float32)
    out = {}
    for k, v in d.items():
        if k == 'v':
            out['v_bytes'] = e4m3fn_bytes(x0 / s.astype(np.float64))
            out['v_scale'] = s
        else:
            out[k] = v
    return out


def reference(x, v_bytes, v_scale, mu, gain, u, b_words, b_scales):
    return core(x, e4m3fn_values(v_bytes) * v_scale.astype(np.float64), mu, gain, u, b_words, b_scales)

from contextlib import ExitStack

import concourse.mybir as mybir
from concourse.masks import make_identity

F32 = mybir.dt.float32
BF16 = mybir.dt.bfloat16
I32 = mybir.dt.int32
U32 = mybir.dt.uint32
U8 = mybir.dt.uint8
FP8 = mybir.dt.float8_e4m3fn
FP8X4 = mybir.dt.float8_e4m3fn_x4
FP4X4 = mybir.dt.float4_e2m1fn_x4
MULT = mybir.AluOpType.mult
SUB = mybir.AluOpType.subtract
COPY = mybir.ActivationFunctionType.Copy

M, K, N, R = 1024, 2048, 1024, 512
FLOPS = 2 * (M * K * N + R * M * N + M * N * K)

P = 128
T4 = 4
KG = K // 512
NB = M // 512
NH = N // 512
ACC = 6
IO = 12


def tile_two_sided_image_basis_s8_kernel(tc, x, v_bytes, v_scale, mu, gain, u, b_words, b_scales, out_c, out_z):
    nc = tc.nc
    with ExitStack() as ctx:
        keep = ctx.enter_context(tc.tile_pool(name="keep", bufs=1))
        work = ctx.enter_context(tc.tile_pool(name="work", bufs=2))
        psum = ctx.enter_context(tc.psum_pool(name="psum", bufs=1))

        ident = keep.tile([P, P], F32, name="ident")
        make_identity(nc, ident[:])
        ones = keep.tile([P, P], BF16, name="ones")
        nc.vector.memset(ones[:], 1.0)
        gz = keep.tile([P, N], BF16, name="gz")
        nc.vector.memset(gz[:].bitcast(I32), 0)
        warm = keep.tile([P, 1], F32, name="warm")
        nc.vector.memset(warm[:], 0.0)
        warm2 = keep.tile([P, 1], F32, name="warm2")
        nc.scalar.activation(out=warm2[:], in_=warm[:], func=COPY, scale=warm[:])
        bs = keep.tile([P, NH, K], U8, name="bs", align_bytes=64)
        nc.gpsimd.memset(bs[:].rearrange("p g n -> p (g n)").bitcast(I32), 0)

        sc = keep.tile([P, KG, 8], F32, name="sc")
        nc.scalar.dma_start(out=sc[:, :, 0:4], in_=v_scale.rearrange("(g p t) o -> p g (t o)", p=P, t=T4))
        nc.scalar.dma_start(out=gz[0:1, :], in_=gain.rearrange("(o n) -> o n", o=1))

        vb = [None] * KG
        xs = {}
        mus = [None] * NB

        def load_v(g):
            vt = work.tile([P, T4, N], U8, name="vb%d" % g, tag="io", bufs=IO)
            nc.sync.dma_start(out=vt[:].rearrange("p t n -> p (t n)"), in_=v_bytes.rearrange("(g p t) n -> g p (t n)", p=P, t=T4)[g])
            vb[g] = vt

        def load_x(b, t):
            xt = work.tile([P, K], BF16, name="xs", tag="io", bufs=IO)
            nc.sync.dma_start(out=xt[:], in_=x.rearrange("(b p t) k -> b p t k", p=P, t=T4)[b][:, t, :])
            xs[b, t] = xt

        def load_mu(b):
            mt = keep.tile([P, T4, N], BF16, name="mu%d" % b)
            nc.sync.dma_start(out=mt[:], in_=mu.rearrange("(b p t) n -> b p t n", p=P, t=T4)[b])
            mus[b] = mt

        load_v(0)
        load_x(0, 0)
        load_x(0, 1)
        load_v(1)
        load_x(0, 2)
        load_v(2)
        load_x(0, 3)
        load_v(3)
        load_x(1, 0)
        load_x(1, 1)
        load_mu(0)
        load_x(1, 2)
        load_x(1, 3)
        load_mu(1)
        us = keep.tile([P, 4, M], BF16, name="uin")
        nc.sync.dma_start(out=us[:], in_=u.rearrange("(j p) m -> p j m", p=P))
        for r in range(4):
            nc.sync.dma_start(
                out=bs[r : 128 : 32, :, :].bitcast(I32),
                in_=b_scales[:, r : 16 : 4, :].rearrange("g q n -> q g n").bitcast(I32),
            )
        bw = keep.tile([P, NH, 2 * K], U8, name="bw", align_bytes=64)
        for g in range(NH):
            nc.sync.dma_start(out=bw[:, g, :], in_=b_words[g])

        vplane, vil, vq, vs = {}, {}, {}, {}

        def widen(g, h, t, on_scalar):
            if (g, h) not in vplane:
                vp_tile = work.tile([P, T4, 512], BF16, name="vp", tag="vp", bufs=3)
                vplane[g, h] = vp_tile
            src = vb[g][:, t, h * 512 : (h + 1) * 512].bitcast(FP8)
            if on_scalar:
                nc.scalar.activation(out=vplane[g, h][:, t, :], in_=src, func=COPY, scale=sc[:, g, t : t + 1])
            else:
                nc.vector.tensor_scalar(out=vplane[g, h][:, t, :], in0=src, scalar1=sc[:, g, t : t + 1], scalar2=None, op0=MULT)

        def interleave(dst, src, on_scalar):
            o = dst[:].rearrange("p (c i) t -> p c t i", i=4)
            i = src[:].rearrange("p t (c i) -> p c t i", i=4)
            if on_scalar:
                nc.scalar.copy(out=o, in_=i)
            else:
                nc.vector.tensor_copy(out=o, in_=i)

        def il_v(g, h, on_scalar=False):
            vi = work.tile([P, 512, T4], BF16, name="vi", tag="vi", bufs=2, align_bytes=64)
            interleave(vi, vplane[g, h], on_scalar)
            vil[g, h] = vi

        def quant(name, src_flat, cols):
            q = keep.tile([P, cols], U32, name=name + "q", align_bytes=64)
            s = keep.tile([P, cols], U8, name=name + "s", align_bytes=64)
            nc.vector.quantize_mx(out=q[:].bitcast(FP8X4), scales=s[:], in_=src_flat)
            return q, s

        def q_v(g, h):
            vq[g, h], vs[g, h] = quant("v%d%d" % (g, h), vil[g, h][:].rearrange("p n t -> p (n t)"), 512)

        def transposes(dst, words, j):
            for a in range(2):
                for e in range(2):
                    first = 256 * (2 * j + a) + e
                    nc.tensor.transpose(dst[:, a, e, :], words[:, first : first + 255 : 2], ident[:])

        def empty(dst, bank, j, on_scalar):
            o = dst[:, 2 * j : 2 * j + 2].rearrange("p a m e -> p (a m e)").bitcast(F32).rearrange("p (a m e) -> p a m e", a=2, e=2)
            i = bank[:].rearrange("p a e m -> p a m e")
            if on_scalar:
                nc.scalar.copy(out=o, in_=i)
            else:
                nc.vector.tensor_copy(out=o, in_=i)

        tbank = {}

        def turn(key, words, j):
            bank = psum.tile([P, 2, 2, P], F32, name="tb", tag="tb", bufs=8 - ACC)
            transposes(bank, words, j)
            tbank[key, j] = bank

        xt4, xq, xsc = {}, {}, {}

        def t_x(b, t, j):
            turn(("x", b, t), xs[b, t][:].bitcast(F32), j)

        def e_x(b, t, j, on_scalar):
            if (b, t) not in xt4:
                xt_tile = work.tile([P, KG, P, T4], BF16, name="xt", tag="xt", bufs=2, align_bytes=64)
                xt4[b, t] = xt_tile
            empty(xt4[b, t], tbank[("x", b, t), j], j, on_scalar)

        def q_x(b, t):
            xq[b, t], xsc[b, t] = quant("x%d%d" % (b, t), xt4[b, t][:].rearrange("p g m t -> p (g m t)"), 512)

        yb = {}

        def y_pass(b, t, h, g):
            if g == 0:
                y_tile = psum.tile([P, 512], F32, name="acc", tag="acc", bufs=ACC)
                yb[b, t, h] = y_tile
            nc.tensor.matmul_mx(
                out=yb[b, t, h][:],
                lhsT=xq[b, t][:, g * 128 : (g + 1) * 128].bitcast(FP8X4),
                lhsT_scale=xsc[b, t][:, g * 128 : (g + 1) * 128],
                rhs=vq[g, h][:].bitcast(FP8X4),
                rhs_scale=vs[g, h][:],
                start=(g == 0),
                stop=(g == KG - 1),
            )

        gb = keep.tile([P, N], F32, name="gb")

        def gain_all():
            for h in range(NH):
                g_tile = psum.tile([P, 512], F32, name="acc", tag="acc", bufs=ACC)
                nc.tensor.matmul(g_tile[:], lhsT=ones[:], rhs=gz[:, h * 512 : (h + 1) * 512], start=True, stop=True)
                nc.vector.tensor_copy(out=gb[:, h * 512 : (h + 1) * 512], in_=g_tile[:])

        dif, hp, hil, hcq, hcs, ht4, hzq, hzs = {}, {}, {}, {}, {}, {}, {}, {}

        def sub(b, t, h):
            d_tile = work.tile([P, 512], F32, name="dif", tag="dif", bufs=6)
            nc.vector.tensor_tensor(out=d_tile[:], in0=yb[b, t, h][:], in1=mus[b][:, t, h * 512 : (h + 1) * 512], op=SUB)
            dif[b, t, h] = d_tile

        def mul(b, t, h):
            if (b, h) not in hp:
                hp_tile = work.tile([P, T4, 512], BF16, name="hp", tag="hp", bufs=4)
                hp[b, h] = hp_tile
            nc.vector.tensor_tensor(out=hp[b, h][:, t, :], in0=dif[b, t, h][:], in1=gb[:, h * 512 : (h + 1) * 512], op=MULT)

        def il_h(b, h, on_scalar):
            hi = work.tile([P, 512, T4], BF16, name="hi", tag="hi", bufs=2, align_bytes=64)
            interleave(hi, hp[b, h], on_scalar)
            hil[b, h] = hi

        def q_hc(b, h):
            hcq[b, h], hcs[b, h] = quant("hc%d%d" % (b, h), hil[b, h][:].rearrange("p n t -> p (n t)"), 512)

        def t_h(b, h, j):
            turn(("h", b, h), hp[b, h][:].rearrange("p t n -> p (t n)").bitcast(F32), j)

        def e_h(b, h, j, on_scalar):
            if (b, h) not in ht4:
                ht_tile = work.tile([P, T4, P, T4], BF16, name="ht", tag="ht", bufs=2, align_bytes=64)
                ht4[b, h] = ht_tile
            empty(ht4[b, h], tbank[("h", b, h), j], j, on_scalar)

        def q_hz(b, h):
            hzq[b, h], hzs[b, h] = quant("hz%d%d" % (b, h), ht4[b, h][:].rearrange("p s m t -> p (s m t)"), 512)

        ut = keep.tile([P, 4, NB, P, T4], BF16, name="ut", align_bytes=64)
        uqs = []

        def t_u(j):
            bank = psum.tile([P, 2, 2, P], F32, name="tb", tag="tb", bufs=8 - ACC)
            transposes(bank, us[:, j, :].bitcast(F32), 0)
            tbank["u", j] = bank

        def e_u(j, on_scalar):
            empty(ut[:, j], tbank["u", j], 0, on_scalar)

        def q_u():
            uqs.extend(quant("u", ut[:].rearrange("p j b r t -> p (j b r t)"), 1024))

        def c_tile(j, h, on_scalar):
            acc = psum.tile([P, 512], F32, name="acc", tag="acc", bufs=ACC)
            for b in range(NB):
                cols = slice((2 * j + b) * 128, (2 * j + b + 1) * 128)
                nc.tensor.matmul_mx(
                    out=acc[:], lhsT=uqs[0][:, cols].bitcast(FP8X4), lhsT_scale=uqs[1][:, cols],
                    rhs=hcq[b, h][:].bitcast(FP8X4), rhs_scale=hcs[b, h][:], start=(b == 0), stop=(b == NB - 1),
                )
            stage = work.tile([P, 512], F32, name="cs", tag="io", bufs=IO)
            if on_scalar:
                nc.scalar.copy(out=stage[:], in_=acc[:])
            else:
                nc.vector.tensor_copy(out=stage[:], in_=acc[:])
            nc.sync.dma_start(out=out_c.rearrange("(j p) n -> j p n", p=P)[j][:, h * 512 : (h + 1) * 512], in_=stage[:])

        zst = {}

        def z_tile(b, t, q, on_scalar):
            acc = psum.tile([P, 512], F32, name="acc", tag="acc", bufs=ACC)
            for h in range(NH):
                nc.tensor.matmul_mx(
                    out=acc[:],
                    lhsT=hzq[b, h][:, t * 128 : (t + 1) * 128].bitcast(FP8X4),
                    lhsT_scale=hzs[b, h][:, t * 128 : (t + 1) * 128],
                    rhs=bw[:, h, q * 1024 : (q + 1) * 1024].bitcast(FP4X4),
                    rhs_scale=bs[:, h, q * 512 : (q + 1) * 512],
                    start=(h == 0), stop=(h == NH - 1),
                )
            half = q // 2
            if (b, t, half) not in zst:
                z_stage = work.tile([P, 1024], F32, name="zs", tag="io", bufs=IO)
                zst[b, t, half] = z_stage
            stage = zst[b, t, half]
            o = stage[:, (q % 2) * 512 : (q % 2 + 1) * 512]
            if on_scalar:
                nc.scalar.copy(out=o, in_=acc[:])
            else:
                nc.vector.tensor_copy(out=o, in_=acc[:])
            if q % 2 == 1:
                nc.sync.dma_start(
                    out=out_z.rearrange("(b p t) k -> b p t k", p=P, t=T4)[b][:, t, half * 1024 : (half + 1) * 1024], in_=stage[:])


        def yx(b, i, h):
            for t in range(i):
                y_pass(b, t, h, i)
            for g in range(i + 1):
                y_pass(b, i, h, g)

        with tc.manual_schedule():
            for i in range(4):
                t_x(0, i, 0)
                t_x(0, i, 1)
                if i:
                    yx(0, i - 1, 0)
                ns = 2 if i == 0 else 3
                for t in range(4):
                    widen(i, 0, t, t < ns)
                e_x(0, i, 0, True)
                e_x(0, i, 1, True)
                il_v(i, 0)
                q_x(0, i)
                q_v(i, 0)
            gain_all()
            for i in range(4):
                t_x(1, i, 0)
                t_x(1, i, 1)
                if i == 0:
                    yx(0, 3, 0)
                else:
                    for g in range(4):
                        y_pass(1, i - 1, 0, g)
                    for t in range(2):
                        y_pass(0, t, 1, i - 1)
                for t in range(4):
                    widen(i, 1, t, True)
                e_x(1, i, 0, True)
                e_x(1, i, 1, True)
                il_v(i, 1)
                sub(0, i, 0)
                q_v(i, 1)
                mul(0, i, 0)
                q_x(1, i)
            sub(1, 0, 0)
            for t in range(2):
                y_pass(0, t, 1, 3)
            for t in range(2, 4):
                for g in range(4):
                    y_pass(0, t, 1, g)
            sub(0, 0, 1)
            sub(0, 1, 1)
            mul(0, 0, 1)
            sub(0, 2, 1)
            mul(0, 1, 1)
            sub(0, 3, 1)
            mul(0, 2, 1)
            t_h(0, 0, 0)
            t_h(0, 0, 1)
            e_h(0, 0, 0, True)
            e_h(0, 0, 1, True)
            sub(1, 1, 0)
            mul(0, 3, 1)
            q_hz(0, 0)
            for g in range(4):
                y_pass(1, 3, 0, g)
            for g in range(4):
                y_pass(1, 0, 1, g)
            t_h(0, 1, 0)
            t_h(0, 1, 1)
            e_h(0, 1, 0, True)
            e_h(0, 1, 1, True)
            sub(1, 2, 0)
            mul(1, 0, 0)
            mul(1, 1, 0)
            q_hz(0, 1)
            sub(1, 3, 0)
            il_h(0, 0, True)
            for t in range(1, 4):
                for g in range(4):
                    y_pass(1, t, 1, g)
            mul(1, 2, 0)
            mul(1, 3, 0)
            for t in range(4):
                sub(1, t, 1)
                if t:
                    mul(1, t - 1, 1)
            il_h(1, 0, False)
            mul(1, 3, 1)
            for t in range(4):
                for q in range(4):
                    z_tile(0, t, q, True)
                    if q == 1 and t == 2:
                        for j in range(2):
                            t_u(j)
                            e_u(j, False)
                        q_hz(1, 0)
                    if q == 1 and t == 3:
                        t_h(1, 1, 0)
                        t_h(1, 1, 1)
                        e_h(1, 1, 0, False)
                        e_h(1, 1, 1, False)
                        q_u()
                if t == 1:
                    t_h(1, 0, 0)
                    t_h(1, 0, 1)
                    e_h(1, 0, 0, False)
                    e_h(1, 0, 1, False)
                    q_hc(0, 0)
                    q_hc(1, 0)
                if t == 2:
                    for j in range(2, 4):
                        t_u(j)
                        e_u(j, False)
                    il_h(0, 1, False)
            q_hz(1, 1)
            for j in range(4):
                c_tile(j, 0, True)
            q_hc(0, 1)
            il_h(1, 1, False)
            for q in range(4):
                z_tile(1, 0, q, q % 2 == 0)
            q_hc(1, 1)
            for q in range(4):
                z_tile(1, 1, q, q % 2 == 0)
            for j in range(4):
                c_tile(j, 1, j % 2 == 0)
            for t in range(2, 4):
                for q in range(4):
                    z_tile(1, t, q, q % 2 == 0)
